import numpy as np
import ml_dtypes


def mxq(x, axis, fmt="e4m3"):
    dtype, down = {"e4m3": (ml_dtypes.float8_e4m3fn, 7), "e5m2": (ml_dtypes.float8_e5m2, 14)}[fmt]
    v = np.moveaxis(np.asarray(x, np.float32).astype(ml_dtypes.bfloat16).astype(np.float64), axis, -1)
    blocks = v.reshape(v.shape[:-1] + (-1, 32))
    amax = np.abs(blocks).max(-1, keepdims=True)
    byte = np.maximum(np.where(amax > 0, np.frexp(amax)[1] - 1 + 127, 0) - down, 1)
    scale = np.exp2(byte - 127.0)
    codes = (blocks / scale).astype(np.float32).astype(dtype).astype(np.float64)
    return np.moveaxis((codes * scale).reshape(v.shape), -1, axis)


WIDE = False


def mx_kscale(k):
    if not WIDE:
        return np.ones(k)
    levels = np.array([10, -10, 5, -5, 0])
    if k % 512:
        return np.exp2(np.random.permutation(np.resize(levels, k // 32))).repeat(32)
    a = np.empty((k // 512, 16))
    for p in range(k // 512):
        a[p, :8] = np.random.permutation(np.resize(levels, 8))
        for g in range(8):
            far = levels[np.abs(levels - a[p, g]) >= 10]
            a[p, g + 8] = far[np.random.randint(len(far))]
    return np.exp2(a.ravel()).repeat(32)


def f64(x):
    return np.asarray(x).astype(np.float64)


def striped(idx):
    return np.tile(idx.reshape(-1, 16).T, (8, 1)).astype(np.uint16)


def unstriped(offs):
    return offs[:16].T.reshape(-1).astype(np.int64)


E2M1 = np.array([0.0, 0.5, 1.0, 1.5, 2.0, 3.0, 4.0, 6.0, -0.0, -0.5, -1.0, -1.5, -2.0, -3.0, -4.0, -6.0])


def pack_weight(w, fmt):
    k, n = w.shape
    w = f64(np.asarray(w, np.float32).astype(ml_dtypes.bfloat16)).reshape(k // 32, 32, n)
    amax = np.abs(w).max(1)
    if fmt == "e4m3":
        byte = np.frexp(amax)[1] - 1 + 127 - 7
    else:
        mant, ex = np.frexp(amax / 6.0)
        byte = np.where(mant > 0.5, ex, ex - 1) + 127
    byte = np.clip(np.where(amax > 0, byte, 1), 1, 254)
    scaled = (w * np.exp2(127.0 - byte)[:, None, :]).reshape(k, n).astype(np.float32)
    by_word = np.ascontiguousarray(scaled.reshape(k // 512, 128, 4, n).transpose(0, 1, 3, 2))
    if fmt == "e4m3":
        words = by_word.astype(ml_dtypes.float8_e4m3fn).view(np.uint8)
    else:
        c = by_word.astype(ml_dtypes.float4_e2m1fn).view(np.uint8) & 0xF
        words = (c[..., 0::2] | (c[..., 1::2] << 4)).reshape(k // 512, 128, 2 * n)
    return np.ascontiguousarray(words), np.ascontiguousarray(byte.astype(np.uint8).reshape(k // 512, 16, n))


def unpack_weight(words, scales, fmt):
    g, _, n = scales.shape
    words = np.ascontiguousarray(words).reshape(g, 128, n, -1)
    if fmt == "e4m3":
        vals = words.view(ml_dtypes.float8_e4m3fn).astype(np.float64)
    else:
        nib = np.empty((g, 128, n, 4), np.uint8)
        nib[..., 0::2] = words & 0xF
        nib[..., 1::2] = words >> 4
        vals = E2M1[nib]
    vals = vals * np.repeat(np.exp2(scales.astype(np.float64) - 127.0), 8, axis=1)[..., None]
    return vals.transpose(0, 1, 3, 2).reshape(g * 512, n)


def silu(v):
    return v / (1.0 + np.exp(-np.maximum(v, -700.0)))


K, T, E, C, D, H, N = 512, 1024, 4, 256, 128, 512, 128


def by_expert(wq, xq, C):
    return np.concatenate([wq[e].T @ xq[:, e * C:(e + 1) * C] for e in range(E)], axis=1)


def setup_inputs():
    n = np.random.standard_normal
    s = mx_kscale(K)
    u = mx_kscale(H)
    first = np.random.permutation(np.repeat(np.arange(E), C))
    slots1 = np.concatenate([np.random.permutation(np.flatnonzero(first == e)) for e in range(E)])
    free = np.ones(T, bool); slots2 = np.empty(E * D, np.int64)
    for e in np.random.permutation(E):
        pick = np.random.permutation(np.flatnonzero(free & (first != e)))[:D]; slots2[e * D:(e + 1) * D] = pick; free[pick] = False
    g1 = np.random.uniform(0.5, 1.0, T); g2 = 1.0 - g1
    x = pack_weight(n((K, T)) * s[:, None], "e4m3")
    return {
        "x_words": x[0],
        "x_scales": x[1],
        "w1": (n((E, K, H)) / np.sqrt(K) / s[None, :, None] * u).astype(np.float32),
        "w2": (n((E, H, N)) / np.sqrt(H) / u[None, :, None]).astype(np.float32),
        "gate1": (np.tile(g1[slots1], (128, 1))).astype(np.float32),
        "gate2": (np.tile(g2[slots2], (128, 1))).astype(np.float32),
        "offs": striped(slots1),
        "offs2": striped(slots2),
    }


def reference(x_words, x_scales, w1, w2, gate1, gate2, offs, offs2):
    w1q = mxq(f64(w1), 1, "e4m3")
    w2q = mxq(f64(w2), 1, "e4m3")
    idx, idx2 = unstriped(offs), unstriped(offs2)
    x = unpack_weight(x_words, x_scales, "e4m3")
    h = silu(by_expert(w1q, x[:, idx], C))
    y = by_expert(w2q, mxq(h, 0, "e4m3"), C)
    h = silu(by_expert(w1q, x[:, idx2], D))
    z = by_expert(w2q, mxq(h, 0, "e4m3"), D)
    out = np.zeros((N, T))
    out[:, idx] = f64(gate1[:1]) * y
    out[:, idx2] += f64(gate2[:1]) * z
    return out

@@ -1,0 +1,216 @@
+from contextlib import ExitStack
+
+import concourse.mybir as mybir
+
+K, T, E, C, D, H, N = 512, 1024, 4, 256, 128, 512, 128
+FLOPS = 2 * E * (C + D) * (K * H + H * N)
+
+F32 = mybir.dt.float32
+BF16 = mybir.dt.bfloat16
+I32 = mybir.dt.int32
+U32 = mybir.dt.uint32
+U16 = mybir.dt.uint16
+U8 = mybir.dt.uint8
+FP8X4 = mybir.dt.float8_e4m3fn_x4
+MULT = mybir.AluOpType.mult
+ADD = mybir.AluOpType.add
+SILU = mybir.ActivationFunctionType.Silu
+
+P = 128
+PACK = 4
+SLOTS = C + D
+BLOCK = 128
+LIST_ROWS = 16
+HALF = H // 2
+
+
+def tile_moe_ada_mlp_silu_kernel(
+    tc, x_words, x_scales, w1, w2, gate1, gate2, offs, offs2, out
+):
+    nc = tc.nc
+    with ExitStack() as ctx:
+        keep = ctx.enter_context(tc.tile_pool(name="keep", bufs=1))
+        ring = ctx.enter_context(tc.tile_pool(name="ring", bufs=2))
+        psum = ctx.enter_context(tc.psum_pool(name="psum", bufs=1))
+
+        list1 = keep.tile([P, E * C // LIST_ROWS], U16, name="list1")
+        list2 = keep.tile([P, E * D // LIST_ROWS], U16, name="list2")
+        token_words = keep.tile([P, T], U32, name="token_words", align_bytes=64)
+        token_scales = keep.tile([P, T], U8, name="token_scales", align_bytes=64)
+        gate1_sb = keep.tile([P, E * C], F32, name="gate1_sb")
+        gate2_sb = keep.tile([P, E * D], F32, name="gate2_sb")
+        first = keep.tile([P, T], F32, name="first")
+        second = keep.tile([P, T], F32, name="second")
+        warm_in = keep.tile([P, 8], F32, name="warm_in")
+        warm_out = keep.tile([P, 8], F32, name="warm_out")
+
+        nc.vector.memset(token_scales[:].bitcast(I32), 0)
+        nc.vector.memset(warm_in[:], 0.0)
+        nc.scalar.activation(warm_out[:], warm_in[:], SILU)
+        nc.vector.memset(second[:], 0.0)
+
+        w1_raw, w2_raw, w1_bf, w2_bf = {}, {}, {}, {}
+        w1_q, w2_q, x_q, h_bf, h_q, pre, acc, y = {}, {}, {}, {}, {}, {}, {}, {}
+
+        def load_w1(e, half):
+            w1_raw[e, half] = ring.tile([P, PACK, HALF], F32, name="w1_raw", bufs=4)
+            rows = w1[e].rearrange("(p j) c -> p j c", j=PACK)
+            nc.sync.dma_start(out=w1_raw[e, half][:], in_=rows[:, :, half * HALF : (half + 1) * HALF])
+
+        def load_w2(e):
+            w2_raw[e] = ring.tile([P, PACK, N], F32, name="w2_raw", bufs=4)
+            nc.sync.dma_start(out=w2_raw[e][:], in_=w2[e].rearrange("(p j) n -> p j n", j=PACK))
+
+        def weave_w1(e, half):
+            if half == 0:
+                w1_bf[e] = ring.tile([P, PACK * H], BF16, name="w1_bf", align_bytes=64)
+            m0, m1 = half * HALF // PACK, (half + 1) * HALF // PACK
+            nc.scalar.copy(
+                w1_bf[e][:].rearrange("p (t m j) -> p m j t", t=PACK, j=PACK)[:, m0:m1],
+                w1_raw[e, half][:].rearrange("p j (m t) -> p m j t", t=PACK),
+            )
+
+        def weave_w2(e):
+            w2_bf[e] = ring.tile([P, PACK * N], BF16, name="w2_bf", align_bytes=64)
+            copy = nc.scalar.copy if e == 0 else nc.vector.tensor_copy
+            copy(
+                w2_bf[e][:].rearrange("p (c i j) -> p c j i", i=4, j=PACK),
+                w2_raw[e][:].rearrange("p j (c i) -> p c j i", i=4),
+            )
+
+        def quantize(name, source, width):
+            codes = ring.tile([P, width], U32, name=name + "_codes", align_bytes=64)
+            scales = ring.tile([P, width], U8, name=name + "_scales", align_bytes=64)
+            nc.vector.quantize_mx(out=codes[:].bitcast(FP8X4), scales=scales[:], in_=source)
+            return codes, scales
+
+        def gather(e):
+            words = ring.tile([P, SLOTS], U32, name="slot_words", align_bytes=64)
+            scales = ring.tile([P, SLOTS], U8, name="slot_scales", align_bytes=64)
+            a = list1[:, e * C // LIST_ROWS : (e + 1) * C // LIST_ROWS]
+            b = list2[:, e * D // LIST_ROWS : (e + 1) * D // LIST_ROWS]
+            nc.vector.tensor_copy(words[:, :C], token_words[:].indirect(a))
+            nc.vector.tensor_copy(words[:, C:], token_words[:].indirect(b))
+            nc.vector.tensor_copy(scales[:, :C], token_scales[:].indirect(a))
+            nc.vector.tensor_copy(scales[:, C:], token_scales[:].indirect(b))
+            x_q[e] = (words, scales)
+
+        def first_layer(e, b):
+            bank = psum.tile([P, PACK, BLOCK], F32, name="bank%d" % b)
+            pre[e, b] = bank
+            cols = slice(b * BLOCK, (b + 1) * BLOCK)
+            for t in range(PACK):
+                ch = slice(t * P, (t + 1) * P)
+                nc.tensor.matmul_mx(
+                    out=bank[:, t, :],
+                    lhsT=w1_q[e][0][:, ch].bitcast(FP8X4),
+                    lhsT_scale=w1_q[e][1][:, ch],
+                    rhs=x_q[e][0][:, cols].bitcast(FP8X4),
+                    rhs_scale=x_q[e][1][:, cols],
+                    start=True,
+                    stop=True,
+                )
+
+        def activate(e, b):
+            if b == 0:
+                h_bf[e, 0] = ring.tile([P, C * PACK], BF16, name="h1_bf", align_bytes=64)
+            if b == 2:
+                h_bf[e, 1] = ring.tile([P, D * PACK], BF16, name="h2_bf", align_bytes=64)
+            dst = h_bf[e, b // 2][:, (b % 2) * BLOCK * PACK : (b % 2 + 1) * BLOCK * PACK]
+            nc.scalar.activation(
+                dst.rearrange("p (s t) -> p s t", t=PACK), pre[e, b][:].rearrange("p t s -> p s t"), SILU
+            )
+
+        def second_layer(e, part):
+            if part == 0:
+                acc[e, part] = psum.tile([P, C], F32, name="acc")
+            else:
+                acc[e, part] = psum.tile([P, D], F32, name="bank0")
+            nc.tensor.matmul_mx(
+                out=acc[e, part][:],
+                lhsT=w2_q[e][0][:].bitcast(FP8X4),
+                lhsT_scale=w2_q[e][1][:],
+                rhs=h_q[e, part][0][:].bitcast(FP8X4),
+                rhs_scale=h_q[e, part][1][:],
+                start=True,
+                stop=True,
+            )
+
+        def leave_psum(e, part):
+            y[e, part] = ring.tile([P, (C, D)[part]], F32, name="y%d" % part)
+            nc.scalar.copy(y[e, part][:], acc[e, part][:])
+
+        def scatter(e, part):
+            width, offsets, window, gate = ((C, list1, first, gate1_sb), (D, list2, second, gate2_sb))[part]
+            entries = offsets[:, e * width // LIST_ROWS : (e + 1) * width // LIST_ROWS]
+            nc.vector.tensor_tensor(
+                window[:].indirect(entries), y[e, part][:], gate[:, e * width : (e + 1) * width], MULT
+            )
+
+        load_w1(0, 0)
+        nc.sync.dma_start(list1[:], offs)
+        nc.sync.dma_start(
+            out=token_words[:].bitcast(I32), in_=x_words[0].rearrange("p t d -> p (t d)").bitcast(I32)
+        )
+        nc.sync.dma_start(list2[:], offs2)
+        scale_rows = x_scales[0].bitcast(I32)
+        for r in range(4):
+            nc.sync.dma_start(out=token_scales[r:P:32, :].bitcast(I32), in_=scale_rows[r:16:4, :])
+        load_w1(0, 1)
+        load_w2(0)
+        load_w1(1, 0)
+        load_w1(1, 1)
+        load_w2(1)
+        nc.sync.dma_start(out=gate1_sb[:], in_=gate1)
+        nc.sync.dma_start(out=gate2_sb[:], in_=gate2)
+        for e in range(2, E):
+            load_w1(e, 0)
+            load_w1(e, 1)
+            load_w2(e)
+
+        weave_w1(0, 0)
+        weave_w1(0, 1)
+        gather(0)
+        gather(1)
+        w1_q[0] = quantize("w1", w1_bf[0][:], H)
+        weave_w2(0)
+        for b in range(3):
+            first_layer(0, b)
+        w2_q[0] = quantize("w2", w2_bf[0][:], N)
+        gather(2)
+        weave_w1(1, 0)
+        for e in range(E):
+            activate(e, 0)
+            if e > 0:
+                second_layer(e - 1, 1)
+            activate(e, 1)
+            h_q[e, 0] = quantize("h1", h_bf[e, 0][:], C)
+            if e > 0:
+                leave_psum(e - 1, 1)
+                scatter(e - 1, 1)
+            second_layer(e, 0)
+            activate(e, 2)
+            h_q[e, 1] = quantize("h2", h_bf[e, 1][:], D)
+            if e + 1 < E:
+                weave_w1(e + 1, 1)
+                weave_w2(e + 1)
+                w1_q[e + 1] = quantize("w1", w1_bf[e + 1][:], H)
+            leave_psum(e, 0)
+            scatter(e, 0)
+            if e + 1 < E:
+                for b in range(3):
+                    first_layer(e + 1, b)
+                w2_q[e + 1] = quantize("w2", w2_bf[e + 1][:], N)
+            if e + 3 < E:
+                gather(e + 3)
+            if e + 2 < E:
+                weave_w1(e + 2, 0)
+        second_layer(E - 1, 1)
+        leave_psum(E - 1, 1)
+        scatter(E - 1, 1)
+
+        for c0 in range(0, T, 512):
+            cols = slice(c0, c0 + 512)
+            total = ring.tile([P, 512], F32, name="total")
+            nc.vector.tensor_tensor(total[:], first[:, cols], second[:, cols], ADD)
+            nc.sync.dma_start(out=out[:, cols], in_=total[:])

@@ -18,10 +18,17 @@ SILU = mybir.ActivationFunctionType.Silu
 
 P = 128
 PACK = 4
-SLOTS = C + D
-BLOCK = 128
+ALIGN = 64
+QUADRANT = 32
 LIST_ROWS = 16
+BLOCK = 128
+BLOCKS = (C + D) // BLOCK
+FIRST, SECOND = 0, 1
+WIDTH = (C, D)
+RUN = 512
 HALF = H // 2
+VECTOR_STAGE = 0
+STORE_EDGES = (0, 512, 768, T)
 
 
 def tile_moe_ada_mlp_silu_kernel(
@@ -33,184 +40,187 @@ def tile_moe_ada_mlp_silu_kernel(
         ring = ctx.enter_context(tc.tile_pool(name="ring", bufs=2))
         psum = ctx.enter_context(tc.psum_pool(name="psum", bufs=1))
 
-        list1 = keep.tile([P, E * C // LIST_ROWS], U16, name="list1")
-        list2 = keep.tile([P, E * D // LIST_ROWS], U16, name="list2")
-        token_words = keep.tile([P, T], U32, name="token_words", align_bytes=64)
-        token_scales = keep.tile([P, T], U8, name="token_scales", align_bytes=64)
-        gate1_sb = keep.tile([P, E * C], F32, name="gate1_sb")
-        gate2_sb = keep.tile([P, E * D], F32, name="gate2_sb")
-        first = keep.tile([P, T], F32, name="first")
-        second = keep.tile([P, T], F32, name="second")
-        warm_in = keep.tile([P, 8], F32, name="warm_in")
-        warm_out = keep.tile([P, 8], F32, name="warm_out")
+        lists = (
+            keep.tile([P, E * C // LIST_ROWS], U16, name="list_first"),
+            keep.tile([P, E * D // LIST_ROWS], U16, name="list_second"),
+        )
+        token_words = keep.tile([P, T], U32, name="token_words", align_bytes=ALIGN)
+        token_scales = keep.tile([P, T], U8, name="token_scales", align_bytes=ALIGN)
+        windows = (keep.tile([P, T], F32, name="window_first"), keep.tile([P, T], F32, name="window_second"))
+        zero = keep.tile([P, 1], F32, name="zero")
 
-        nc.vector.memset(token_scales[:].bitcast(I32), 0)
-        nc.vector.memset(warm_in[:], 0.0)
-        nc.scalar.activation(warm_out[:], warm_in[:], SILU)
-        nc.vector.memset(second[:], 0.0)
+        w1_raw, w2_raw, w1_woven, gates = {}, {}, {}, {}
+        w1_mx, w2_mx, slot_words, slot_scales, h, pre, y_psum = {}, {}, {}, {}, {}, {}, {}
 
-        w1_raw, w2_raw, w1_bf, w2_bf = {}, {}, {}, {}
-        w1_q, w2_q, x_q, h_bf, h_q, pre, acc, y = {}, {}, {}, {}, {}, {}, {}, {}
+        def load_w1(e, c0, c1):
+            raw = keep.tile([P, PACK, c1 - c0], F32, name="w1_raw_%d_%d" % (e, c0), align_bytes=ALIGN)
+            nc.sync.dma_start(out=raw[:], in_=w1[e].rearrange("(p j) c -> p j c", j=PACK)[:, :, c0:c1])
+            w1_raw[e, c0] = raw
 
-        def load_w1(e, half):
-            w1_raw[e, half] = ring.tile([P, PACK, HALF], F32, name="w1_raw", bufs=4)
-            rows = w1[e].rearrange("(p j) c -> p j c", j=PACK)
-            nc.sync.dma_start(out=w1_raw[e, half][:], in_=rows[:, :, half * HALF : (half + 1) * HALF])
-
-        def load_w2(e):
-            w2_raw[e] = ring.tile([P, PACK, N], F32, name="w2_raw", bufs=4)
-            nc.sync.dma_start(out=w2_raw[e][:], in_=w2[e].rearrange("(p j) n -> p j n", j=PACK))
-
-        def weave_w1(e, half):
-            if half == 0:
-                w1_bf[e] = ring.tile([P, PACK * H], BF16, name="w1_bf", align_bytes=64)
-            m0, m1 = half * HALF // PACK, (half + 1) * HALF // PACK
-            nc.scalar.copy(
-                w1_bf[e][:].rearrange("p (t m j) -> p m j t", t=PACK, j=PACK)[:, m0:m1],
-                w1_raw[e, half][:].rearrange("p j (m t) -> p m j t", t=PACK),
+        def load_w2(e0, e1):
+            raw = keep.tile([P, e1 - e0, PACK, N], F32, name="w2_raw_%d" % e0)
+            nc.sync.dma_start(
+                out=raw[:].rearrange("p e j n -> p e (j n)"),
+                in_=w2[e0:e1].rearrange("e (p j) n -> p e (j n)", j=PACK),
             )
+            w2_raw[e0] = raw
 
-        def weave_w2(e):
-            w2_bf[e] = ring.tile([P, PACK * N], BF16, name="w2_bf", align_bytes=64)
-            copy = nc.scalar.copy if e == 0 else nc.vector.tensor_copy
-            copy(
-                w2_bf[e][:].rearrange("p (c i j) -> p c j i", i=4, j=PACK),
-                w2_raw[e][:].rearrange("p j (c i) -> p c j i", i=4),
-            )
+        def load_gates(e0, e1):
+            for choice, gate in ((FIRST, gate1), (SECOND, gate2)):
+                width = WIDTH[choice]
+                tile = keep.tile([P, (e1 - e0) * width], F32, name="gate_%d_%d" % (choice, e0))
+                nc.sync.dma_start(out=tile[:], in_=gate[:, e0 * width : e1 * width])
+                for e in range(e0, e1):
+                    gates[e, choice] = tile[:, (e - e0) * width : (e - e0 + 1) * width]
 
-        def quantize(name, source, width):
-            codes = ring.tile([P, width], U32, name=name + "_codes", align_bytes=64)
-            scales = ring.tile([P, width], U8, name=name + "_scales", align_bytes=64)
+        def entries(choice, a0, a1):
+            return lists[choice][:, a0 // LIST_ROWS : a1 // LIST_ROWS]
+
+        def gather(source, dtype, gathered, choice, a0, tag):
+            tile = keep.tile([P, RUN], dtype, name=tag, align_bytes=ALIGN)
+            nc.vector.tensor_copy(tile[:], source[:].indirect(entries(choice, a0, a0 + RUN)))
+            for s0 in range(0, RUN, BLOCK):
+                e, within = divmod(a0 + s0, WIDTH[choice])
+                gathered[e, (choice * C + within) // BLOCK] = tile[:, s0 : s0 + BLOCK]
+
+        def quantize(pool, name, source, width):
+            codes = pool.tile([P, width], U32, name=name + "_codes", align_bytes=ALIGN)
+            scales = pool.tile([P, width], U8, name=name + "_scales", align_bytes=ALIGN)
             nc.vector.quantize_mx(out=codes[:].bitcast(FP8X4), scales=scales[:], in_=source)
             return codes, scales
 
-        def gather(e):
-            words = ring.tile([P, SLOTS], U32, name="slot_words", align_bytes=64)
-            scales = ring.tile([P, SLOTS], U8, name="slot_scales", align_bytes=64)
-            a = list1[:, e * C // LIST_ROWS : (e + 1) * C // LIST_ROWS]
-            b = list2[:, e * D // LIST_ROWS : (e + 1) * D // LIST_ROWS]
-            nc.vector.tensor_copy(words[:, :C], token_words[:].indirect(a))
-            nc.vector.tensor_copy(words[:, C:], token_words[:].indirect(b))
-            nc.vector.tensor_copy(scales[:, :C], token_scales[:].indirect(a))
-            nc.vector.tensor_copy(scales[:, C:], token_scales[:].indirect(b))
-            x_q[e] = (words, scales)
+        def weave_w1(e, c0, c1, copy):
+            if c0 == 0:
+                w1_woven[e] = keep.tile([P, PACK * H], BF16, name="w1_woven_%d" % e, align_bytes=ALIGN)
+            copy(
+                w1_woven[e][:].rearrange("p (t m j) -> p m j t", t=PACK, j=PACK)[:, c0 // PACK : c1 // PACK],
+                w1_raw[e, c0][:].rearrange("p j (m t) -> p m j t", t=PACK),
+            )
 
         def first_layer(e, b):
-            bank = psum.tile([P, PACK, BLOCK], F32, name="bank%d" % b)
-            pre[e, b] = bank
-            cols = slice(b * BLOCK, (b + 1) * BLOCK)
+            pre[e, b] = psum.tile([P, PACK, BLOCK], F32, name="pre_%d" % b, bufs=2)
+            codes, scales = w1_mx[e]
             for t in range(PACK):
-                ch = slice(t * P, (t + 1) * P)
+                columns = slice(t * P, (t + 1) * P)
                 nc.tensor.matmul_mx(
-                    out=bank[:, t, :],
-                    lhsT=w1_q[e][0][:, ch].bitcast(FP8X4),
-                    lhsT_scale=w1_q[e][1][:, ch],
-                    rhs=x_q[e][0][:, cols].bitcast(FP8X4),
-                    rhs_scale=x_q[e][1][:, cols],
+                    out=pre[e, b][:, t, :],
+                    lhsT=codes[:, columns].bitcast(FP8X4),
+                    lhsT_scale=scales[:, columns],
+                    rhs=slot_words[e, b].bitcast(FP8X4),
+                    rhs_scale=slot_scales[e, b],
                     start=True,
                     stop=True,
                 )
 
+        def prepare_w1(e, copy):
+            weave_w1(e, 0, H, copy)
+            w1_mx[e] = quantize(keep, "w1_%d" % e, w1_woven[e][:], H)
+            for b in range(BLOCKS):
+                first_layer(e, b)
+
+        def prepare_w2(e0, e1, copy):
+            woven = keep.tile([P, (e1 - e0) * PACK * N], BF16, name="w2_woven_%d" % e0, align_bytes=ALIGN)
+            copy(
+                woven[:].rearrange("p (e c i j) -> p e c j i", e=e1 - e0, i=PACK, j=PACK),
+                w2_raw[e0][:].rearrange("p e j (c i) -> p e c j i", i=PACK),
+            )
+            codes, scales = quantize(keep, "w2_%d" % e0, woven[:], (e1 - e0) * N)
+            for e in range(e0, e1):
+                columns = slice((e - e0) * N, (e - e0 + 1) * N)
+                w2_mx[e] = (codes[:, columns], scales[:, columns])
+
         def activate(e, b):
-            if b == 0:
-                h_bf[e, 0] = ring.tile([P, C * PACK], BF16, name="h1_bf", align_bytes=64)
-            if b == 2:
-                h_bf[e, 1] = ring.tile([P, D * PACK], BF16, name="h2_bf", align_bytes=64)
-            dst = h_bf[e, b // 2][:, (b % 2) * BLOCK * PACK : (b % 2 + 1) * BLOCK * PACK]
+            choice, s0 = divmod(b * BLOCK, C)
+            if s0 == 0:
+                shape = [P, WIDTH[choice] * PACK]
+                if choice == FIRST and e + 1 in woven_on_scalar:
+                    h[e, choice] = keep.tile(shape, BF16, name="w1_raw_%d_0" % (e + 1), align_bytes=ALIGN)
+                else:
+                    h[e, choice] = ring.tile(shape, BF16, name="h_%d" % choice, align_bytes=ALIGN)
             nc.scalar.activation(
-                dst.rearrange("p (s t) -> p s t", t=PACK), pre[e, b][:].rearrange("p t s -> p s t"), SILU
+                h[e, choice][:, s0 * PACK : (s0 + BLOCK) * PACK].rearrange("p (s t) -> p s t", t=PACK),
+                pre[e, b][:].rearrange("p t s -> p s t"),
+                SILU,
             )
 
-        def second_layer(e, part):
-            if part == 0:
-                acc[e, part] = psum.tile([P, C], F32, name="acc")
-            else:
-                acc[e, part] = psum.tile([P, D], F32, name="bank0")
+        def second_layer(e, choice):
+            codes, scales = quantize(ring, "h_%d" % choice, h[e, choice][:], WIDTH[choice])
+            y_psum[e, choice] = psum.tile([P, WIDTH[choice]], F32, name="y_psum_%d" % choice)
             nc.tensor.matmul_mx(
-                out=acc[e, part][:],
-                lhsT=w2_q[e][0][:].bitcast(FP8X4),
-                lhsT_scale=w2_q[e][1][:],
-                rhs=h_q[e, part][0][:].bitcast(FP8X4),
-                rhs_scale=h_q[e, part][1][:],
+                out=y_psum[e, choice][:],
+                lhsT=w2_mx[e][0].bitcast(FP8X4),
+                lhsT_scale=w2_mx[e][1],
+                rhs=codes[:].bitcast(FP8X4),
+                rhs_scale=scales[:],
                 start=True,
                 stop=True,
             )
 
-        def leave_psum(e, part):
-            y[e, part] = ring.tile([P, (C, D)[part]], F32, name="y%d" % part)
-            nc.scalar.copy(y[e, part][:], acc[e, part][:])
+        def scatter(e, choice):
+            width = WIDTH[choice]
+            y = ring.tile([P, width], F32, name="y_%d" % choice)
+            nc.scalar.copy(y[:], y_psum[e, choice][:])
+            target = windows[choice][:].indirect(entries(choice, e * width, (e + 1) * width))
+            nc.vector.tensor_tensor(target, y[:], gates[e, choice], MULT)
 
-        def scatter(e, part):
-            width, offsets, window, gate = ((C, list1, first, gate1_sb), (D, list2, second, gate2_sb))[part]
-            entries = offsets[:, e * width // LIST_ROWS : (e + 1) * width // LIST_ROWS]
-            nc.vector.tensor_tensor(
-                window[:].indirect(entries), y[e, part][:], gate[:, e * width : (e + 1) * width], MULT
+        w2_of_stage = ((1, 2), (2, E))
+        woven_on_scalar = [e for e in range(E) if e != VECTOR_STAGE + 2]
+
+        nc.vector.memset(token_scales[:].bitcast(I32), 0)
+        nc.vector.memset(zero[:], 0.0)
+
+        nc.sync.dma_start(lists[FIRST][:], offs)
+        nc.sync.dma_start(out=token_words[:].bitcast(I32), in_=x_words[0].rearrange("p t d -> p (t d)").bitcast(I32))
+        nc.sync.dma_start(lists[SECOND][:], offs2)
+        load_w1(0, 0, HALF)
+        for r in range(PACK):
+            nc.sync.dma_start(
+                out=token_scales[r:P:QUADRANT, :].bitcast(I32), in_=x_scales[0].bitcast(I32)[r : K // 32 : PACK, :]
             )
+        load_w1(0, HALF, H)
+        nc.scalar.activation(windows[SECOND][:], zero[:].to_broadcast([P, T]), SILU)
+        for e in range(1, E):
+            load_w1(e, 0, H)
+            if e < E - 1:
+                load_w2(e - 1, e)
+        load_gates(0, E // 2)
+        load_w2(*w2_of_stage[1])
+        load_gates(E // 2, E)
 
-        load_w1(0, 0)
-        nc.sync.dma_start(list1[:], offs)
-        nc.sync.dma_start(
-            out=token_words[:].bitcast(I32), in_=x_words[0].rearrange("p t d -> p (t d)").bitcast(I32)
-        )
-        nc.sync.dma_start(list2[:], offs2)
-        scale_rows = x_scales[0].bitcast(I32)
-        for r in range(4):
-            nc.sync.dma_start(out=token_scales[r:P:32, :].bitcast(I32), in_=scale_rows[r:16:4, :])
-        load_w1(0, 1)
-        load_w2(0)
-        load_w1(1, 0)
-        load_w1(1, 1)
-        load_w2(1)
-        nc.sync.dma_start(out=gate1_sb[:], in_=gate1)
-        nc.sync.dma_start(out=gate2_sb[:], in_=gate2)
-        for e in range(2, E):
-            load_w1(e, 0)
-            load_w1(e, 1)
-            load_w2(e)
+        for choice, a0 in ((FIRST, 0), (SECOND, 0), (FIRST, RUN)):
+            gather(token_words, U32, slot_words, choice, a0, "slot_words_%d_%d" % (choice, a0))
+        gather(token_scales, U8, slot_scales, FIRST, 0, "slot_scales")
+        weave_w1(0, 0, HALF, nc.scalar.copy)
+        weave_w1(0, HALF, H, nc.scalar.copy)
+        w1_mx[0] = quantize(keep, "w1_0", w1_woven[0][:], H)
+        first_layer(0, 0)
+        first_layer(0, 1)
+        gather(token_scales, U8, slot_scales, SECOND, 0, "w1_raw_0_%d" % HALF)
+        gather(token_scales, U8, slot_scales, FIRST, RUN, "w1_woven_0")
+        first_layer(0, 2)
+        prepare_w1(1, nc.scalar.copy)
+        prepare_w2(0, 1, nc.scalar.copy)
 
-        weave_w1(0, 0)
-        weave_w1(0, 1)
-        gather(0)
-        gather(1)
-        w1_q[0] = quantize("w1", w1_bf[0][:], H)
-        weave_w2(0)
-        for b in range(3):
-            first_layer(0, b)
-        w2_q[0] = quantize("w2", w2_bf[0][:], N)
-        gather(2)
-        weave_w1(1, 0)
         for e in range(E):
             activate(e, 0)
-            if e > 0:
-                second_layer(e - 1, 1)
             activate(e, 1)
-            h_q[e, 0] = quantize("h1", h_bf[e, 0][:], C)
-            if e > 0:
-                leave_psum(e - 1, 1)
-                scatter(e - 1, 1)
-            second_layer(e, 0)
+            second_layer(e, FIRST)
+            if e == E - 1:
+                scatter(e - 1, FIRST)
+            elif e > 0:
+                scatter(e - 1, SECOND)
             activate(e, 2)
-            h_q[e, 1] = quantize("h2", h_bf[e, 1][:], D)
-            if e + 1 < E:
-                weave_w1(e + 1, 1)
-                weave_w2(e + 1)
-                w1_q[e + 1] = quantize("w1", w1_bf[e + 1][:], H)
-            leave_psum(e, 0)
-            scatter(e, 0)
-            if e + 1 < E:
-                for b in range(3):
-                    first_layer(e + 1, b)
-                w2_q[e + 1] = quantize("w2", w2_bf[e + 1][:], N)
-            if e + 3 < E:
-                gather(e + 3)
-            if e + 2 < E:
-                weave_w1(e + 2, 0)
-        second_layer(E - 1, 1)
-        leave_psum(E - 1, 1)
-        scatter(E - 1, 1)
+            second_layer(e, SECOND)
+            if e < len(w2_of_stage):
+                copy = nc.vector.tensor_copy if e == VECTOR_STAGE else nc.scalar.copy
+                prepare_w2(*w2_of_stage[e], copy)
+                prepare_w1(e + 2, copy)
+                scatter(e, FIRST)
+        scatter(E - 2, SECOND)
+        scatter(E - 1, FIRST)
+        scatter(E - 1, SECOND)
 
-        for c0 in range(0, T, 512):
-            cols = slice(c0, c0 + 512)
-            total = ring.tile([P, 512], F32, name="total")
-            nc.vector.tensor_tensor(total[:], first[:, cols], second[:, cols], ADD)
-            nc.sync.dma_start(out=out[:, cols], in_=total[:])
+        for c0, c1 in zip(STORE_EDGES, STORE_EDGES[1:]):
+            total = keep.tile([P, c1 - c0], F32, name="total_%d" % c0)
+            nc.vector.tensor_tensor(total[:], windows[FIRST][:, c0:c1], windows[SECOND][:, c0:c1], ADD)
+            nc.sync.dma_start(out=out[:, c0:c1], in_=total[:])

from contextlib import ExitStack

import concourse.mybir as mybir

K, T, E, C, D, H, N = 512, 1024, 4, 256, 128, 512, 128
FLOPS = 2 * E * (C + D) * (K * H + H * N)

F32 = mybir.dt.float32
BF16 = mybir.dt.bfloat16
I32 = mybir.dt.int32
U32 = mybir.dt.uint32
U16 = mybir.dt.uint16
U8 = mybir.dt.uint8
FP8X4 = mybir.dt.float8_e4m3fn_x4
MULT = mybir.AluOpType.mult
ADD = mybir.AluOpType.add
SILU = mybir.ActivationFunctionType.Silu

P = 128
PACK = 4
ALIGN = 64
QUADRANT = 32
LIST_ROWS = 16
BLOCK = 128
BLOCKS = (C + D) // BLOCK
FIRST, SECOND = 0, 1
WIDTH = (C, D)
RUN = 512
HALF = H // 2
VECTOR_STAGE = 0
STORE_EDGES = (0, 512, 768, T)


def tile_moe_ada_mlp_silu_kernel(
    tc, x_words, x_scales, w1, w2, gate1, gate2, offs, offs2, out
):
    nc = tc.nc
    with ExitStack() as ctx:
        keep = ctx.enter_context(tc.tile_pool(name="keep", bufs=1))
        ring = ctx.enter_context(tc.tile_pool(name="ring", bufs=2))
        psum = ctx.enter_context(tc.psum_pool(name="psum", bufs=1))

        lists = (
            keep.tile([P, E * C // LIST_ROWS], U16, name="list_first"),
            keep.tile([P, E * D // LIST_ROWS], U16, name="list_second"),
        )
        token_words = keep.tile([P, T], U32, name="token_words", align_bytes=ALIGN)
        token_scales = keep.tile([P, T], U8, name="token_scales", align_bytes=ALIGN)
        windows = (keep.tile([P, T], F32, name="window_first"), keep.tile([P, T], F32, name="window_second"))
        zero = keep.tile([P, 1], F32, name="zero")

        w1_raw, w2_raw, w1_woven, gates = {}, {}, {}, {}
        w1_mx, w2_mx, slot_words, slot_scales, h, pre, y_psum = {}, {}, {}, {}, {}, {}, {}

        def load_w1(e, c0, c1):
            raw = keep.tile([P, PACK, c1 - c0], F32, name="w1_raw_%d_%d" % (e, c0), align_bytes=ALIGN)
            nc.sync.dma_start(out=raw[:], in_=w1[e].rearrange("(p j) c -> p j c", j=PACK)[:, :, c0:c1])
            w1_raw[e, c0] = raw

        def load_w2(e0, e1):
            raw = keep.tile([P, e1 - e0, PACK, N], F32, name="w2_raw_%d" % e0)
            nc.sync.dma_start(
                out=raw[:].rearrange("p e j n -> p e (j n)"),
                in_=w2[e0:e1].rearrange("e (p j) n -> p e (j n)", j=PACK),
            )
            w2_raw[e0] = raw

        def load_gates(e0, e1):
            for choice, gate in ((FIRST, gate1), (SECOND, gate2)):
                width = WIDTH[choice]
                tile = keep.tile([P, (e1 - e0) * width], F32, name="gate_%d_%d" % (choice, e0))
                nc.sync.dma_start(out=tile[:], in_=gate[:, e0 * width : e1 * width])
                for e in range(e0, e1):
                    gates[e, choice] = tile[:, (e - e0) * width : (e - e0 + 1) * width]

        def entries(choice, a0, a1):
            return lists[choice][:, a0 // LIST_ROWS : a1 // LIST_ROWS]

        def gather(source, dtype, gathered, choice, a0, tag):
            tile = keep.tile([P, RUN], dtype, name=tag, align_bytes=ALIGN)
            nc.vector.tensor_copy(tile[:], source[:].indirect(entries(choice, a0, a0 + RUN)))
            for s0 in range(0, RUN, BLOCK):
                e, within = divmod(a0 + s0, WIDTH[choice])
                gathered[e, (choice * C + within) // BLOCK] = tile[:, s0 : s0 + BLOCK]

        def quantize(pool, name, source, width):
            codes = pool.tile([P, width], U32, name=name + "_codes", align_bytes=ALIGN)
            scales = pool.tile([P, width], U8, name=name + "_scales", align_bytes=ALIGN)
            nc.vector.quantize_mx(out=codes[:].bitcast(FP8X4), scales=scales[:], in_=source)
            return codes, scales

        def weave_w1(e, c0, c1, copy):
            if c0 == 0:
                w1_woven[e] = keep.tile([P, PACK * H], BF16, name="w1_woven_%d" % e, align_bytes=ALIGN)
            copy(
                w1_woven[e][:].rearrange("p (t m j) -> p m j t", t=PACK, j=PACK)[:, c0 // PACK : c1 // PACK],
                w1_raw[e, c0][:].rearrange("p j (m t) -> p m j t", t=PACK),
            )

        def first_layer(e, b):
            pre[e, b] = psum.tile([P, PACK, BLOCK], F32, name="pre_%d" % b, bufs=2)
            codes, scales = w1_mx[e]
            for t in range(PACK):
                columns = slice(t * P, (t + 1) * P)
                nc.tensor.matmul_mx(
                    out=pre[e, b][:, t, :],
                    lhsT=codes[:, columns].bitcast(FP8X4),
                    lhsT_scale=scales[:, columns],
                    rhs=slot_words[e, b].bitcast(FP8X4),
                    rhs_scale=slot_scales[e, b],
                    start=True,
                    stop=True,
                )

        def prepare_w1(e, copy):
            weave_w1(e, 0, H, copy)
            w1_mx[e] = quantize(keep, "w1_%d" % e, w1_woven[e][:], H)
            for b in range(BLOCKS):
                first_layer(e, b)

        def prepare_w2(e0, e1, copy):
            woven = keep.tile([P, (e1 - e0) * PACK * N], BF16, name="w2_woven_%d" % e0, align_bytes=ALIGN)
            copy(
                woven[:].rearrange("p (e c i j) -> p e c j i", e=e1 - e0, i=PACK, j=PACK),
                w2_raw[e0][:].rearrange("p e j (c i) -> p e c j i", i=PACK),
            )
            codes, scales = quantize(keep, "w2_%d" % e0, woven[:], (e1 - e0) * N)
            for e in range(e0, e1):
                columns = slice((e - e0) * N, (e - e0 + 1) * N)
                w2_mx[e] = (codes[:, columns], scales[:, columns])

        def activate(e, b):
            choice, s0 = divmod(b * BLOCK, C)
            if s0 == 0:
                shape = [P, WIDTH[choice] * PACK]
                if choice == FIRST and e + 1 in woven_on_scalar:
                    h[e, choice] = keep.tile(shape, BF16, name="w1_raw_%d_0" % (e + 1), align_bytes=ALIGN)
                else:
                    h[e, choice] = ring.tile(shape, BF16, name="h_%d" % choice, align_bytes=ALIGN)
            nc.scalar.activation(
                h[e, choice][:, s0 * PACK : (s0 + BLOCK) * PACK].rearrange("p (s t) -> p s t", t=PACK),
                pre[e, b][:].rearrange("p t s -> p s t"),
                SILU,
            )

        def second_layer(e, choice):
            codes, scales = quantize(ring, "h_%d" % choice, h[e, choice][:], WIDTH[choice])
            y_psum[e, choice] = psum.tile([P, WIDTH[choice]], F32, name="y_psum_%d" % choice)
            nc.tensor.matmul_mx(
                out=y_psum[e, choice][:],
                lhsT=w2_mx[e][0].bitcast(FP8X4),
                lhsT_scale=w2_mx[e][1],
                rhs=codes[:].bitcast(FP8X4),
                rhs_scale=scales[:],
                start=True,
                stop=True,
            )

        def scatter(e, choice):
            width = WIDTH[choice]
            y = ring.tile([P, width], F32, name="y_%d" % choice)
            nc.scalar.copy(y[:], y_psum[e, choice][:])
            target = windows[choice][:].indirect(entries(choice, e * width, (e + 1) * width))
            nc.vector.tensor_tensor(target, y[:], gates[e, choice], MULT)

        w2_of_stage = ((1, 2), (2, E))
        woven_on_scalar = [e for e in range(E) if e != VECTOR_STAGE + 2]

        nc.vector.memset(token_scales[:].bitcast(I32), 0)
        nc.vector.memset(zero[:], 0.0)

        nc.sync.dma_start(lists[FIRST][:], offs)
        nc.sync.dma_start(out=token_words[:].bitcast(I32), in_=x_words[0].rearrange("p t d -> p (t d)").bitcast(I32))
        nc.sync.dma_start(lists[SECOND][:], offs2)
        load_w1(0, 0, HALF)
        for r in range(PACK):
            nc.sync.dma_start(
                out=token_scales[r:P:QUADRANT, :].bitcast(I32), in_=x_scales[0].bitcast(I32)[r : K // 32 : PACK, :]
            )
        load_w1(0, HALF, H)
        nc.scalar.activation(windows[SECOND][:], zero[:].to_broadcast([P, T]), SILU)
        for e in range(1, E):
            load_w1(e, 0, H)
            if e < E - 1:
                load_w2(e - 1, e)
        load_gates(0, E // 2)
        load_w2(*w2_of_stage[1])
        load_gates(E // 2, E)

        for choice, a0 in ((FIRST, 0), (SECOND, 0), (FIRST, RUN)):
            gather(token_words, U32, slot_words, choice, a0, "slot_words_%d_%d" % (choice, a0))
        gather(token_scales, U8, slot_scales, FIRST, 0, "slot_scales")
        weave_w1(0, 0, HALF, nc.scalar.copy)
        weave_w1(0, HALF, H, nc.scalar.copy)
        w1_mx[0] = quantize(keep, "w1_0", w1_woven[0][:], H)
        first_layer(0, 0)
        first_layer(0, 1)
        gather(token_scales, U8, slot_scales, SECOND, 0, "w1_raw_0_%d" % HALF)
        gather(token_scales, U8, slot_scales, FIRST, RUN, "w1_woven_0")
        first_layer(0, 2)
        prepare_w1(1, nc.scalar.copy)
        prepare_w2(0, 1, nc.scalar.copy)

        for e in range(E):
            activate(e, 0)
            activate(e, 1)
            second_layer(e, FIRST)
            if e == E - 1:
                scatter(e - 1, FIRST)
            elif e > 0:
                scatter(e - 1, SECOND)
            activate(e, 2)
            second_layer(e, SECOND)
            if e < len(w2_of_stage):
                copy = nc.vector.tensor_copy if e == VECTOR_STAGE else nc.scalar.copy
                prepare_w2(*w2_of_stage[e], copy)
                prepare_w1(e + 2, copy)
                scatter(e, FIRST)
        scatter(E - 2, SECOND)
        scatter(E - 1, FIRST)
        scatter(E - 1, SECOND)

        for c0, c1 in zip(STORE_EDGES, STORE_EDGES[1:]):
            total = keep.tile([P, c1 - c0], F32, name="total_%d" % c0)
            nc.vector.tensor_tensor(total[:], windows[FIRST][:, c0:c1], windows[SECOND][:, c0:c1], ADD)
            nc.sync.dma_start(out=out[:, c0:c1], in_=total[:])
